import numpy as np
import ml_dtypes


def mxq(x, axis, fmt="e4m3"):
    dtype, down = {"e4m3": (ml_dtypes.float8_e4m3fn, 7), "e5m2": (ml_dtypes.float8_e5m2, 14)}[fmt]
    v = np.moveaxis(np.asarray(x, np.float32).astype(ml_dtypes.bfloat16).astype(np.float64), axis, -1)
    blocks = v.reshape(v.shape[:-1] + (-1, 32))
    amax = np.abs(blocks).max(-1, keepdims=True)
    byte = np.maximum(np.where(amax > 0, np.frexp(amax)[1] - 1 + 127, 0) - down, 1)
    scale = np.exp2(byte - 127.0)
    codes = (blocks / scale).astype(np.float32).astype(dtype).astype(np.float64)
    return np.moveaxis((codes * scale).reshape(v.shape), -1, axis)


WIDE = False


def mx_kscale(k):
    if not WIDE:
        return np.ones(k)
    levels = np.array([10, -10, 5, -5, 0])
    if k % 512:
        return np.exp2(np.random.permutation(np.resize(levels, k // 32))).repeat(32)
    a = np.empty((k // 512, 16))
    for p in range(k // 512):
        a[p, :8] = np.random.permutation(np.resize(levels, 8))
        for g in range(8):
            far = levels[np.abs(levels - a[p, g]) >= 10]
            a[p, g + 8] = far[np.random.randint(len(far))]
    return np.exp2(a.ravel()).repeat(32)


def f64(x):
    return np.asarray(x).astype(np.float64)


def striped(idx):
    return np.tile(idx.reshape(-1, 16).T, (8, 1)).astype(np.uint16)


def unstriped(offs):
    return offs[:16].T.reshape(-1).astype(np.int64)


E2M1 = np.array([0.0, 0.5, 1.0, 1.5, 2.0, 3.0, 4.0, 6.0, -0.0, -0.5, -1.0, -1.5, -2.0, -3.0, -4.0, -6.0])


def pack_weight(w, fmt):
    k, n = w.shape
    w = f64(np.asarray(w, np.float32).astype(ml_dtypes.bfloat16)).reshape(k // 32, 32, n)
    amax = np.abs(w).max(1)
    if fmt == "e4m3":
        byte = np.frexp(amax)[1] - 1 + 127 - 7
    else:
        mant, ex = np.frexp(amax / 6.0)
        byte = np.where(mant > 0.5, ex, ex - 1) + 127
    byte = np.clip(np.where(amax > 0, byte, 1), 1, 254)
    scaled = (w * np.exp2(127.0 - byte)[:, None, :]).reshape(k, n).astype(np.float32)
    by_word = np.ascontiguousarray(scaled.reshape(k // 512, 128, 4, n).transpose(0, 1, 3, 2))
    if fmt == "e4m3":
        words = by_word.astype(ml_dtypes.float8_e4m3fn).view(np.uint8)
    else:
        c = by_word.astype(ml_dtypes.float4_e2m1fn).view(np.uint8) & 0xF
        words = (c[..., 0::2] | (c[..., 1::2] << 4)).reshape(k // 512, 128, 2 * n)
    return np.ascontiguousarray(words), np.ascontiguousarray(byte.astype(np.uint8).reshape(k // 512, 16, n))


def unpack_weight(words, scales, fmt):
    g, _, n = scales.shape
    words = np.ascontiguousarray(words).reshape(g, 128, n, -1)
    if fmt == "e4m3":
        vals = words.view(ml_dtypes.float8_e4m3fn).astype(np.float64)
    else:
        nib = np.empty((g, 128, n, 4), np.uint8)
        nib[..., 0::2] = words & 0xF
        nib[..., 1::2] = words >> 4
        vals = E2M1[nib]
    vals = vals * np.repeat(np.exp2(scales.astype(np.float64) - 127.0), 8, axis=1)[..., None]
    return vals.transpose(0, 1, 3, 2).reshape(g * 512, n)


def gelu(v):
    return 0.5 * v * (1.0 + np.tanh(np.sqrt(2.0 / np.pi) * (v + 0.044715 * v**3)))


def striped8(idx):
    return np.concatenate([v.reshape(-1, 16).T for v in idx]).astype(np.uint16)


def unstriped8(offs):
    return np.stack([offs[16 * g:16 * g + 16].T.reshape(-1) for g in range(8)]).astype(np.int64)


def runs(v, idx8):
    k = np.arange(v.shape[0])
    return v[k[:, None], idx8[k % 512 // 64]]


K, M, H, N, T, S, T2 = 1024, 512, 1024, 512, 2048, 512, 1024

def setup_inputs():
    n = np.random.standard_normal
    s = mx_kscale(K)[:, None]
    s2 = mx_kscale(M)[:, None]
    u = mx_kscale(H)[:, None]
    tab_words, tab_scales = pack_weight(n((K, T)) * s, "e4m3")
    tab2_words, tab2_scales = pack_weight(n((M, T)) * s2, "e4m3")
    w2_words, w2_scales = pack_weight(0.33 * n((M, H)) / np.sqrt(M) / s2, "e2m1")
    w4_words, w4_scales = pack_weight(3.0 * n((H, N)) / np.sqrt(H) / u, "e4m3")
    return {
        "tab_words": tab_words, "tab_scales": tab_scales,
        "tab2_words": tab2_words, "tab2_scales": tab2_scales,
        "offs": striped8(np.stack([np.random.permutation(T)[:S] for _ in range(8)])),
        "offs2": striped(np.random.permutation(T)[:S]),
        "offs3": striped(np.random.permutation(T2)[:S]),
        "w1": (0.33 * n((K, H)) / np.sqrt(K) / s).astype(np.float32),
        "w2_words": w2_words, "w2_scales": w2_scales,
        "w3": (n((M, H)) / np.sqrt(M) / s2).astype(np.float32),
        "w4_words": w4_words, "w4_scales": w4_scales,
        "phase": np.random.uniform(-0.4, 0.4, H).astype(np.float32),
        "gain": (np.random.uniform(0.6, 1.6, H) * u[:, 0]).astype(np.float32),
        "wgo": np.exp(0.3 * n((128, S))).astype(np.float32),
        "page1": n((N, T2)).astype(np.float32),
    }

def reference(tab_words, tab_scales, tab2_words, tab2_scales, offs, offs2, offs3, w1, w2_words, w2_scales, w3, w4_words, w4_scales, phase, gain, wgo, page1):
    v = runs(unpack_weight(tab_words, tab_scales, "e4m3"), unstriped8(offs))
    v2 = unpack_weight(tab2_words, tab2_scales, "e4m3")[:, unstriped(offs2)]
    w2 = unpack_weight(w2_words, w2_scales, "e2m1")
    w4 = unpack_weight(w4_words, w4_scales, "e4m3")
    a = mxq(f64(w1), 0, "e4m3").T @ v + w2.T @ v2
    d = mxq(f64(w3), 0, "e4m3").T @ v2
    wave = np.sin(a + f64(phase)[:, None])
    h = wave / (1.0 + np.square(d)) * f64(gain)[:, None]
    y = w4.T @ mxq(h, 0, "e4m3")
    out = f64(page1).copy()
    out[:, unstriped(offs3)] = np.tile(f64(wgo), (N // 128, 1)) * y
    return out

@@ -1,0 +1,328 @@
+import math
+from contextlib import ExitStack
+
+import concourse.mybir as mybir
+
+K, M, H, N, T, S, T2 = 1024, 512, 1024, 512, 2048, 512, 1024
+FLOPS = 2 * S * (K * H + 2 * M * H + H * N)
+
+F32 = mybir.dt.float32
+BF16 = mybir.dt.bfloat16
+I32 = mybir.dt.int32
+U32 = mybir.dt.uint32
+U16 = mybir.dt.uint16
+U8 = mybir.dt.uint8
+E4M3 = mybir.dt.float8_e4m3fn_x4
+E2M1 = mybir.dt.float4_e2m1fn_x4
+ACT = mybir.ActivationFunctionType
+ALU = mybir.AluOpType
+
+P = 128
+PACK = 4
+KP = P * PACK
+HALF = S // 2
+QUARTER = S // 4
+BLOCKS = H // KP
+TINY = 1e-30
+
+
+def tile_list_rack_patch_features_kernel(
+    tc, tab_words, tab_scales, tab2_words, tab2_scales, offs, offs2, offs3, w1, w2_words, w2_scales,
+    w3, w4_words, w4_scales, phase, gain, wgo, page1, out,
+):
+    nc = tc.nc
+    with ExitStack() as ctx:
+        keep = ctx.enter_context(tc.tile_pool(name="keep", bufs=1))
+        ring = ctx.enter_context(tc.tile_pool(name="ring", bufs=2))
+        psum = ctx.enter_context(tc.psum_pool(name="psum", bufs=1))
+
+        def sb(name, shape, dtype):
+            return keep.tile(shape, dtype, name=name, align_bytes=64)
+
+        list1 = sb("list1", [P, S // 16], U16)
+        list2 = sb("list2", [P, S // 16], U16)
+        list3 = sb("list3", [P, S // 16], U16)
+        tab_w = [sb("tab_w%d" % a, [P, T], U32) for a in range(2)]
+        tab2_w = sb("tab2_w", [P, T], U32)
+        tab_s = sb("tab_s", [P, T], U8)
+        tab2_s = sb("tab2_s", [P, T], U8)
+        w2_w = sb("w2_w", [P, 2 * H], U8)
+        w2_s = sb("w2_s", [P, H], U8)
+        w4_w = [sb("w4_w%d" % b, [P, N], U32) for b in range(BLOCKS)]
+        w4_s = sb("w4_s", [P, N], U8)
+        phase_sb = sb("phase_sb", [P, BLOCKS, PACK], F32)
+        gain_sb = sb("gain_sb", [P, BLOCKS, PACK], F32)
+        wgo_sb = sb("wgo_sb", [P, S], F32)
+        pages = [sb("page%d" % n, [P, T2], F32) for n in range(N // P)]
+
+        nc.vector.memset(tab2_s[:].bitcast(I32), 0)
+        nc.vector.memset(tab_s[:].bitcast(I32), 0)
+        nc.vector.memset(w2_s[:].bitcast(I32), 0)
+        nc.vector.memset(w4_s[:].bitcast(I32), 0)
+
+        raw = {}
+
+        def load_weight(name, w, a, b):
+            raw[name] = sb("raw_" + name, [P, PACK, KP], F32)
+            rows = w[a * KP : (a + 1) * KP, b * KP : (b + 1) * KP]
+            nc.sync.dma_start(out=raw[name][:], in_=rows.rearrange("(p j) c -> p j c", j=PACK))
+
+        codes = {}
+        planes = {}
+
+        def quantise_weight(name, scalar_share):
+            grouped = keep.tile([P, KP * PACK], BF16, name="grouped_" + name, tag="bf_" + name, align_bytes=64)
+            dst = grouped[:].rearrange("p (t m j) -> p m j t", t=PACK, j=PACK)
+            src = raw[name][:].rearrange("p j (m t) -> p m j t", t=PACK)
+            cut = P - scalar_share
+            nc.vector.tensor_copy(out=dst[:, :cut], in_=src[:, :cut])
+            if scalar_share:
+                nc.scalar.copy(out=dst[:, cut:], in_=src[:, cut:])
+            codes[name] = sb("codes_" + name, [P, KP], U32)
+            planes[name] = sb("plane_" + name, [P, KP], U8)
+            nc.vector.quantize_mx(out=codes[name][:].bitcast(E4M3), scales=planes[name][:], in_=grouped[:])
+
+        def words_of(dram, a):
+            return dram[a].rearrange("p t i -> p (t i)").bitcast(I32)
+
+        def load_scale_rows(tile, scales, quadrants):
+            for d in quadrants:
+                nc.sync.dma_start(
+                    out=tile[32 * d : 32 * d + 4, :].bitcast(I32), in_=scales[0, 4 * d : 4 * d + 4, :].bitcast(I32)
+                )
+
+        def load_tab_scales(a):
+            for e in range(2):
+                nc.sync.dma_start(
+                    out=tab_s[4 * a + e : P : 16, :].bitcast(I32), in_=tab_scales[a, e:16:2, :].bitcast(I32)
+                )
+
+        nc.sync.dma_start(list2[:], offs2)
+        nc.sync.dma_start(out=gain_sb[:], in_=gain.rearrange("(b p t) -> p b t", p=P, t=PACK))
+        nc.sync.dma_start(list1[:], offs)
+        load_weight("w3_0", w3, 0, 0)
+        load_scale_rows(tab2_s, tab2_scales, range(4))
+        nc.sync.dma_start(out=tab2_w[:].bitcast(I32), in_=words_of(tab2_words, 0))
+        load_tab_scales(0)
+        load_tab_scales(1)
+        nc.sync.dma_start(out=w2_w[:].bitcast(I32), in_=w2_words[0].bitcast(I32))
+        load_weight("w3_1", w3, 0, 1)
+        nc.sync.dma_start(out=tab_w[0][:].bitcast(I32), in_=words_of(tab_words, 0))
+        load_scale_rows(w2_s, w2_scales, range(2))
+        nc.sync.dma_start(out=tab_w[1][:].bitcast(I32), in_=words_of(tab_words, 1))
+        load_scale_rows(w2_s, w2_scales, range(2, 4))
+
+        def small(name):
+            return sb(name, [P, BLOCKS, PACK], F32)
+
+        half_sign = small("half_sign")
+        nc.vector.tensor_scalar(half_sign[:], gain_sb[:], 0.0, -0.5, ALU.is_ge, ALU.add)
+        half_gain = small("half_gain")
+        nc.vector.tensor_tensor(half_gain[:], gain_sb[:], half_sign[:], ALU.mult)
+        twice_gain = small("twice_gain")
+        nc.vector.tensor_scalar(twice_gain[:], half_gain[:], 4.0, TINY, ALU.mult, ALU.max)
+        gain_root = small("gain_root")
+        nc.scalar.activation(gain_root[:], twice_gain[:], ACT.Abs_reciprocal_sqrt)
+        guess = small("guess")
+        nc.vector.tensor_tensor(guess[:], gain_root[:], gain_root[:], ALU.mult)
+        near_one = small("near_one")
+        nc.vector.tensor_tensor(near_one[:], guess[:], twice_gain[:], ALU.mult)
+        mend = small("mend")
+        nc.vector.tensor_scalar(mend[:], near_one[:], -1.0, 2.0, ALU.mult, ALU.add)
+        inv_gain = small("inv_gain")
+        nc.vector.tensor_tensor(inv_gain[:], guess[:], mend[:], ALU.mult)
+
+        v2_w = sb("v2_w", [P, S], U32)
+        v2_s = sb("v2_s", [P, S], U8)
+        nc.vector.tensor_copy(v2_s[:], tab2_s[:].indirect(list2[:]))
+        quantise_weight("w3_0", 64)
+        nc.vector.tensor_copy(v2_w[:], tab2_w[:].indirect(list2[:]))
+        picked_s = sb("picked_s", [P, S], U8)
+        nc.vector.tensor_copy(picked_s[:], tab_s[:].indirect(list1[:]))
+        v_s = sb("v_s", [P, S], U8)
+        nc.vector.tensor_copy(v_s[:].bitcast(I32), picked_s[:].bitcast(I32))
+
+        def move_odd_row(a, e):
+            nc.sync.dma_start(
+                out=v_s[4 * a + 2 + e : P : 32, :].bitcast(I32),
+                in_=picked_s[16 + 4 * a + e : P : 32, :].bitcast(I32),
+            )
+
+        def load_w4_scales(quadrants):
+            for d in quadrants:
+                nc.sync.dma_start(
+                    out=w4_s[32 * d : 32 * d + 8, :].bitcast(I32), in_=w4_scales[:, 4 * d : 4 * d + 4, :].bitcast(I32)
+                )
+
+        move_odd_row(0, 0)
+        load_weight("w1_00", w1, 0, 0)
+        move_odd_row(0, 1)
+        move_odd_row(1, 0)
+        load_weight("w1_10", w1, 1, 0)
+        move_odd_row(1, 1)
+        nc.sync.dma_start(out=phase_sb[:], in_=phase.rearrange("(b p t) -> p b t", p=P, t=PACK))
+
+        w2_dealt = sb("w2_dealt", [P, 2 * H], U8)
+        w2_dealt_s = sb("w2_dealt_s", [P, H], U8)
+        nc.scalar.copy(
+            out=w2_dealt[:].bitcast(U16).rearrange("p (b t m) -> p b t m", b=BLOCKS, t=PACK),
+            in_=w2_w[:].bitcast(U16).rearrange("p (b m t) -> p b t m", b=BLOCKS, t=PACK),
+        )
+        quantise_weight("w3_1", 0)
+
+        load_weight("w1_01", w1, 0, 1)
+        load_w4_scales(range(2))
+        load_weight("w1_11", w1, 1, 1)
+        load_w4_scales(range(2, 4))
+        for b in range(BLOCKS):
+            nc.sync.dma_start(out=w4_w[b][:].bitcast(I32), in_=words_of(w4_words, b))
+        nc.sync.dma_start(list3[:], offs3)
+        for n in range(N // P):
+            nc.sync.dma_start(out=pages[n][:], in_=page1[n * P : (n + 1) * P, :])
+            if n == 0:
+                nc.sync.dma_start(out=wgo_sb[:], in_=wgo)
+
+        def bank(i):
+            return psum.tile([P, S], F32, name="bank", tag="bank%d" % i)
+
+        def planar(ap):
+            return ap.rearrange("p t (c i) -> p c t i", i=4)
+
+        def woven(ap):
+            return ap.rearrange("p (c i t) -> p c t i", i=4, t=PACK)
+
+        v_w = [sb("v_w%d" % a, [P, S], U32) for a in range(2)]
+        for a in range(2):
+            nc.vector.tensor_copy(v_w[a][:], tab_w[a][:].indirect(list1[:]))
+
+        roots = []
+        damp = {}
+        for b in range(BLOCKS):
+            root = sb("root%d" % b, [P, PACK, S], F32)
+            roots.append(root)
+            for t in range(PACK):
+                cols = slice(t * P, (t + 1) * P)
+                d_ps = bank(4 + t)
+                nc.tensor.matmul_mx(
+                    out=d_ps[:], lhsT=codes["w3_%d" % b][:, cols].bitcast(E4M3), lhsT_scale=planes["w3_%d" % b][:, cols],
+                    rhs=v2_w[:].bitcast(E4M3), rhs_scale=v2_s[:], start=True, stop=True,
+                )
+                d_sq = ring.tile([P, S], F32, name="d_sq")
+                nc.scalar.activation(d_sq[:], d_ps[:], ACT.Square)
+                inv = inv_gain[:, b, t : t + 1]
+                nc.scalar.activation(root[:, t, :], d_sq[:], ACT.Abs_reciprocal_sqrt, bias=inv, scale=inv)
+
+        def damping(b, j0, j1, tag):
+            tile = keep.tile([P, (j1 - j0) * PACK], F32, name="damp", tag=tag, align_bytes=64)
+            nc.scalar.activation(woven(tile[:]), planar(roots[b][:, :, j0:j1]), ACT.Square)
+            for j in range(j0, j1, QUARTER):
+                damp[b, j] = tile[:, PACK * (j - j0) :]
+
+        for b in range(BLOCKS):
+            damping(b, 0, HALF, "damp%d" % b)
+
+        nc.vector.tensor_copy(
+            out=w2_dealt_s[:].rearrange("p (b t m) -> p b t m", b=BLOCKS, t=PACK),
+            in_=w2_s[:].rearrange("p (b m t) -> p b t m", b=BLOCKS, t=PACK),
+        )
+
+        half_phase = sb("half_phase", [P, BLOCKS, PACK], F32)
+        nc.gpsimd.tensor_tensor(half_phase[:], phase_sb[:], half_sign[:], ALU.mult)
+        angle_bias = sb("angle_bias", [P, BLOCKS, PACK], F32)
+        nc.gpsimd.tensor_scalar(angle_bias[:], half_phase[:], math.pi / 4, None, ALU.add)
+
+        h_w = [sb("h_w%d" % b, [P, S], U32) for b in range(BLOCKS)]
+        h_s = [sb("h_s%d" % b, [P, S], U8) for b in range(BLOCKS)]
+
+        def first_product(b, j0, j1, first_bank):
+            width = j1 - j0
+            per_bank = S // width
+            sums = []
+            for g in range(PACK // per_bank):
+                acc = bank(first_bank + g)
+                ts = range(g * per_bank, (g + 1) * per_bank)
+                outs = [acc[:, i * width : (i + 1) * width] for i in range(per_bank)]
+                for i, t in enumerate(ts):
+                    c0 = b * KP + t * P
+                    nc.tensor.matmul_mx(
+                        out=outs[i], lhsT=w2_dealt[:, 2 * c0 : 2 * (c0 + P)].bitcast(E2M1),
+                        lhsT_scale=w2_dealt_s[:, c0 : c0 + P],
+                        rhs=v2_w[:, j0:j1].bitcast(E4M3), rhs_scale=v2_s[:, j0:j1], start=(i == 0), stop=False,
+                    )
+                for a in range(2):
+                    name = "w1_%d%d" % (a, b)
+                    for i, t in enumerate(ts):
+                        cols = slice(t * P, (t + 1) * P)
+                        nc.tensor.matmul_mx(
+                            out=outs[i], lhsT=codes[name][:, cols].bitcast(E4M3), lhsT_scale=planes[name][:, cols],
+                            rhs=v_w[a][:, j0:j1].bitcast(E4M3), rhs_scale=v_s[4 * a :, j0:j1],
+                            start=False, stop=(a == 1 and i == per_bank - 1),
+                        )
+                sums.extend(outs)
+            return sums
+
+        def features(b, sums, j0, j1, sine_tag, rounded):
+            width = j1 - j0
+            sine = keep.tile([P, PACK, width], F32, name="sine", tag=sine_tag, align_bytes=64)
+            for t in range(PACK):
+                nc.scalar.activation(
+                    sine[:, t, :], sums[t], ACT.Sin, bias=angle_bias[:, b, t : t + 1], scale=half_sign[:, b, t : t + 1]
+                )
+            sine_sq = keep.tile([P, width * PACK], F32, name="sine_sq", tag="sq%d_%d" % (b, j0), align_bytes=64)
+            nc.scalar.activation(woven(sine_sq[:]), planar(sine[:]), ACT.Square)
+            nc.vector.scalar_tensor_tensor(
+                rounded, sine_sq[:], -0.5, damp[b, j0][:, : PACK * width], ALU.add, ALU.mult
+            )
+            nc.vector.quantize_mx(out=h_w[b][:, j0:j1].bitcast(E4M3), scales=h_s[b][:, j0:j1], in_=rounded)
+
+        def second_product(j0, bank_index):
+            y_ps = bank(bank_index)
+            for n in range(N // P):
+                cols = slice(n * P, (n + 1) * P)
+                for b in range(BLOCKS):
+                    nc.tensor.matmul_mx(
+                        out=y_ps[:, cols], lhsT=w4_w[b][:, cols].bitcast(E4M3), lhsT_scale=w4_s[4 * b :, cols],
+                        rhs=h_w[b][:, j0 : j0 + QUARTER].bitcast(E4M3), rhs_scale=h_s[b][:, j0 : j0 + QUARTER],
+                        start=(b == 0), stop=(b == BLOCKS - 1),
+                    )
+            return y_ps
+
+        def place(y_ps, j0, n0, n1, tag):
+            y_sb = keep.tile([P, (n1 - n0) * P], F32, name="y_sb", tag=tag, align_bytes=64)
+            nc.scalar.copy(out=y_sb[:], in_=y_ps[:, n0 * P : n1 * P])
+            for n in range(n0, n1):
+                nc.vector.tensor_tensor(
+                    pages[n][:].indirect(list3[:, j0 // 16 : (j0 + QUARTER) // 16]),
+                    y_sb[:, (n - n0) * P : (n - n0 + 1) * P], wgo_sb[:, j0 : j0 + QUARTER], ALU.mult,
+                )
+
+        for name in ("w1_00", "w1_10", "w1_01", "w1_11"):
+            quantise_weight(name, 0)
+        Q = QUARTER
+        sums00 = first_product(0, 0, HALF, 0)
+        sums1 = [first_product(1, q * Q, (q + 1) * Q, 4 + q) for q in range(2)]
+        sums01 = first_product(0, HALF, S, 2)
+        sums1.extend(first_product(1, q * Q, (q + 1) * Q, 4 + q) for q in range(2, 4))
+        h0_bf = keep.tile([P, S * PACK], BF16, name="h0_bf", tag="bf_w1_11", align_bytes=64)
+        h1_bf = sb("h1_bf", [P, S * PACK], BF16)
+        features(0, sums00, 0, HALF, "sine_a", h0_bf[:, 0:1024])
+        features(1, sums1[0], 0, Q, "sine_b", h1_bf[:, 0:512])
+        y0 = second_product(0, 0)
+        features(1, sums1[1], Q, 2 * Q, "sine_a", h1_bf[:, 512:1024])
+        place(y0, 0, 0, 4, "y0")
+        y1 = second_product(Q, 1)
+        place(y1, Q, 0, 2, "y1")
+        damping(0, HALF, S, "sq1_0")
+        features(0, sums01, HALF, S, "sine_b", h0_bf[:, 1024:2048])
+        damping(1, 2 * Q, 3 * Q, "sq1_128")
+        features(1, sums1[2], 2 * Q, 3 * Q, "sine_c", h1_bf[:, 1024:1536])
+        place(y1, Q, 2, 4, "sine_c")
+        y2 = second_product(2 * Q, 2)
+        damping(1, 3 * Q, S, "sq0_256")
+        features(1, sums1[3], 3 * Q, S, "sine_b", h1_bf[:, 1536:2048])
+        place(y2, 2 * Q, 0, 2, "y2")
+        place(y2, 2 * Q, 2, 4, "sine_b")
+        y3 = second_product(3 * Q, 3)
+        place(y3, 3 * Q, 0, 4, "y3")
+        for n in range(N // P):
+            nc.sync.dma_start(out=out[n * P : (n + 1) * P, :], in_=pages[n][:])

@@ -42,7 +42,7 @@ def tile_list_rack_patch_features_kernel(
         list1 = sb("list1", [P, S // 16], U16)
         list2 = sb("list2", [P, S // 16], U16)
         list3 = sb("list3", [P, S // 16], U16)
-        tab_w = [sb("tab_w%d" % a, [P, T], U32) for a in range(2)]
+        tab_w = [keep.tile([P, T], U32, name="tab_w", tag="tab_w%d" % a, align_bytes=64) for a in range(2)]
         tab2_w = sb("tab2_w", [P, T], U32)
         tab_s = sb("tab_s", [P, T], U8)
         tab2_s = sb("tab2_s", [P, T], U8)
@@ -85,11 +85,9 @@ def tile_list_rack_patch_features_kernel(
         def words_of(dram, a):
             return dram[a].rearrange("p t i -> p (t i)").bitcast(I32)
 
-        def load_scale_rows(tile, scales, quadrants):
-            for d in quadrants:
-                nc.sync.dma_start(
-                    out=tile[32 * d : 32 * d + 4, :].bitcast(I32), in_=scales[0, 4 * d : 4 * d + 4, :].bitcast(I32)
-                )
+        def load_scale_rows(tile, scales, rows):
+            for r in rows:
+                nc.sync.dma_start(out=tile[r:P:32, :].bitcast(I32), in_=scales[0, r:16:4, :].bitcast(I32))
 
         def load_tab_scales(a):
             for e in range(2):
@@ -102,10 +100,10 @@ def tile_list_rack_patch_features_kernel(
         nc.sync.dma_start(list1[:], offs)
         load_weight("w3_0", w3, 0, 0)
         load_scale_rows(tab2_s, tab2_scales, range(4))
+        nc.sync.dma_start(out=w2_w[:].bitcast(I32), in_=w2_words[0].bitcast(I32))
         nc.sync.dma_start(out=tab2_w[:].bitcast(I32), in_=words_of(tab2_words, 0))
         load_tab_scales(0)
         load_tab_scales(1)
-        nc.sync.dma_start(out=w2_w[:].bitcast(I32), in_=w2_words[0].bitcast(I32))
         load_weight("w3_1", w3, 0, 1)
         nc.sync.dma_start(out=tab_w[0][:].bitcast(I32), in_=words_of(tab_words, 0))
         load_scale_rows(w2_s, w2_scales, range(2))
@@ -116,21 +114,21 @@ def tile_list_rack_patch_features_kernel(
             return sb(name, [P, BLOCKS, PACK], F32)
 
         half_sign = small("half_sign")
-        nc.vector.tensor_scalar(half_sign[:], gain_sb[:], 0.0, -0.5, ALU.is_ge, ALU.add)
+        nc.gpsimd.tensor_scalar(half_sign[:], gain_sb[:], 0.0, -0.5, ALU.is_ge, ALU.add)
         half_gain = small("half_gain")
-        nc.vector.tensor_tensor(half_gain[:], gain_sb[:], half_sign[:], ALU.mult)
+        nc.gpsimd.tensor_tensor(half_gain[:], gain_sb[:], half_sign[:], ALU.mult)
         twice_gain = small("twice_gain")
-        nc.vector.tensor_scalar(twice_gain[:], half_gain[:], 4.0, TINY, ALU.mult, ALU.max)
-        gain_root = small("gain_root")
+        nc.gpsimd.tensor_scalar(twice_gain[:], half_gain[:], 4.0, TINY, ALU.mult, ALU.max)
+        gain_root = keep.tile([P, BLOCKS, PACK], F32, name="gain_root", tag="bf_w3_0", align_bytes=64)
         nc.scalar.activation(gain_root[:], twice_gain[:], ACT.Abs_reciprocal_sqrt)
         guess = small("guess")
-        nc.vector.tensor_tensor(guess[:], gain_root[:], gain_root[:], ALU.mult)
+        nc.gpsimd.tensor_tensor(guess[:], gain_root[:], gain_root[:], ALU.mult)
         near_one = small("near_one")
-        nc.vector.tensor_tensor(near_one[:], guess[:], twice_gain[:], ALU.mult)
+        nc.gpsimd.tensor_tensor(near_one[:], guess[:], twice_gain[:], ALU.mult)
         mend = small("mend")
-        nc.vector.tensor_scalar(mend[:], near_one[:], -1.0, 2.0, ALU.mult, ALU.add)
+        nc.gpsimd.tensor_scalar(mend[:], near_one[:], -1.0, 2.0, ALU.mult, ALU.add)
         inv_gain = small("inv_gain")
-        nc.vector.tensor_tensor(inv_gain[:], guess[:], mend[:], ALU.mult)
+        nc.gpsimd.tensor_tensor(inv_gain[:], guess[:], mend[:], ALU.mult)
 
         v2_w = sb("v2_w", [P, S], U32)
         v2_s = sb("v2_s", [P, S], U8)
@@ -207,19 +205,23 @@ def tile_list_rack_patch_features_kernel(
                     out=d_ps[:], lhsT=codes["w3_%d" % b][:, cols].bitcast(E4M3), lhsT_scale=planes["w3_%d" % b][:, cols],
                     rhs=v2_w[:].bitcast(E4M3), rhs_scale=v2_s[:], start=True, stop=True,
                 )
-                d_sq = ring.tile([P, S], F32, name="d_sq")
+                d_sq = ring.tile([P, S], F32, name="d_sq", bufs=4)
                 nc.scalar.activation(d_sq[:], d_ps[:], ACT.Square)
                 inv = inv_gain[:, b, t : t + 1]
                 nc.scalar.activation(root[:, t, :], d_sq[:], ACT.Abs_reciprocal_sqrt, bias=inv, scale=inv)
 
-        def damping(b, j0, j1, tag):
+        def damping(b, j0, j1, tag, on_vector=False):
             tile = keep.tile([P, (j1 - j0) * PACK], F32, name="damp", tag=tag, align_bytes=64)
-            nc.scalar.activation(woven(tile[:]), planar(roots[b][:, :, j0:j1]), ACT.Square)
+            root = planar(roots[b][:, :, j0:j1])
+            if on_vector:
+                nc.vector.tensor_tensor(woven(tile[:]), root, root, ALU.mult)
+            else:
+                nc.scalar.activation(woven(tile[:]), root, ACT.Square)
             for j in range(j0, j1, QUARTER):
                 damp[b, j] = tile[:, PACK * (j - j0) :]
 
-        for b in range(BLOCKS):
-            damping(b, 0, HALF, "damp%d" % b)
+        damping(0, 0, HALF, "tab_w1", on_vector=True)
+        damping(1, 0, HALF, "damp10")
 
         nc.vector.tensor_copy(
             out=w2_dealt_s[:].rearrange("p (b t m) -> p b t m", b=BLOCKS, t=PACK),
@@ -227,9 +229,9 @@ def tile_list_rack_patch_features_kernel(
         )
 
         half_phase = sb("half_phase", [P, BLOCKS, PACK], F32)
-        nc.gpsimd.tensor_tensor(half_phase[:], phase_sb[:], half_sign[:], ALU.mult)
+        nc.vector.tensor_tensor(half_phase[:], phase_sb[:], half_sign[:], ALU.mult)
         angle_bias = sb("angle_bias", [P, BLOCKS, PACK], F32)
-        nc.gpsimd.tensor_scalar(angle_bias[:], half_phase[:], math.pi / 4, None, ALU.add)
+        nc.vector.tensor_scalar(angle_bias[:], half_phase[:], math.pi / 4, None, ALU.add)
 
         h_w = [sb("h_w%d" % b, [P, S], U32) for b in range(BLOCKS)]
         h_s = [sb("h_s%d" % b, [P, S], U8) for b in range(BLOCKS)]
@@ -275,54 +277,54 @@ def tile_list_rack_patch_features_kernel(
             )
             nc.vector.quantize_mx(out=h_w[b][:, j0:j1].bitcast(E4M3), scales=h_s[b][:, j0:j1], in_=rounded)
 
-        def second_product(j0, bank_index):
+        def second_product(j0, j1, n0, n1, bank_index):
+            width = j1 - j0
             y_ps = bank(bank_index)
-            for n in range(N // P):
+            for n in range(n0, n1):
                 cols = slice(n * P, (n + 1) * P)
                 for b in range(BLOCKS):
                     nc.tensor.matmul_mx(
-                        out=y_ps[:, cols], lhsT=w4_w[b][:, cols].bitcast(E4M3), lhsT_scale=w4_s[4 * b :, cols],
-                        rhs=h_w[b][:, j0 : j0 + QUARTER].bitcast(E4M3), rhs_scale=h_s[b][:, j0 : j0 + QUARTER],
+                        out=y_ps[:, (n - n0) * width : (n - n0 + 1) * width],
+                        lhsT=w4_w[b][:, cols].bitcast(E4M3), lhsT_scale=w4_s[4 * b :, cols],
+                        rhs=h_w[b][:, j0:j1].bitcast(E4M3), rhs_scale=h_s[b][:, j0:j1],
                         start=(b == 0), stop=(b == BLOCKS - 1),
                     )
             return y_ps
 
-        def place(y_ps, j0, n0, n1, tag):
-            y_sb = keep.tile([P, (n1 - n0) * P], F32, name="y_sb", tag=tag, align_bytes=64)
-            nc.scalar.copy(out=y_sb[:], in_=y_ps[:, n0 * P : n1 * P])
+        def place(values, j0, j1, n0, n1, tag):
+            width = j1 - j0
+            y_sb = keep.tile([P, (n1 - n0) * width], F32, name="y_sb", tag=tag, align_bytes=64)
+            nc.scalar.copy(out=y_sb[:], in_=values)
             for n in range(n0, n1):
                 nc.vector.tensor_tensor(
-                    pages[n][:].indirect(list3[:, j0 // 16 : (j0 + QUARTER) // 16]),
-                    y_sb[:, (n - n0) * P : (n - n0 + 1) * P], wgo_sb[:, j0 : j0 + QUARTER], ALU.mult,
+                    pages[n][:].indirect(list3[:, j0 // 16 : j1 // 16]),
+                    y_sb[:, (n - n0) * width : (n - n0 + 1) * width], wgo_sb[:, j0:j1], ALU.mult,
                 )
 
         for name in ("w1_00", "w1_10", "w1_01", "w1_11"):
             quantise_weight(name, 0)
         Q = QUARTER
         sums00 = first_product(0, 0, HALF, 0)
-        sums1 = [first_product(1, q * Q, (q + 1) * Q, 4 + q) for q in range(2)]
+        sums10 = first_product(1, 0, Q, 4)
+        sums11 = first_product(1, Q, HALF, 5)
         sums01 = first_product(0, HALF, S, 2)
-        sums1.extend(first_product(1, q * Q, (q + 1) * Q, 4 + q) for q in range(2, 4))
+        sums12 = first_product(1, HALF, S, 6)
         h0_bf = keep.tile([P, S * PACK], BF16, name="h0_bf", tag="bf_w1_11", align_bytes=64)
         h1_bf = sb("h1_bf", [P, S * PACK], BF16)
         features(0, sums00, 0, HALF, "sine_a", h0_bf[:, 0:1024])
-        features(1, sums1[0], 0, Q, "sine_b", h1_bf[:, 0:512])
-        y0 = second_product(0, 0)
-        features(1, sums1[1], Q, 2 * Q, "sine_a", h1_bf[:, 512:1024])
-        place(y0, 0, 0, 4, "y0")
-        y1 = second_product(Q, 1)
-        place(y1, Q, 0, 2, "y1")
-        damping(0, HALF, S, "sq1_0")
+        damping(0, HALF, S, "damp01")
+        features(1, sums10, 0, Q, "sine_b", h1_bf[:, 0:512])
+        damping(1, HALF, S, "sq1_0", on_vector=True)
+        y0 = second_product(0, Q, 0, 4, 0)
+        features(1, sums11, Q, HALF, "sine_a", h1_bf[:, 512:1024])
+        place(y0[:], 0, Q, 0, 4, "y0")
+        y1 = second_product(Q, HALF, 0, 4, 1)
+        place(y1[:, :Q], Q, HALF, 0, 1, "y1")
         features(0, sums01, HALF, S, "sine_b", h0_bf[:, 1024:2048])
-        damping(1, 2 * Q, 3 * Q, "sq1_128")
-        features(1, sums1[2], 2 * Q, 3 * Q, "sine_c", h1_bf[:, 1024:1536])
-        place(y1, Q, 2, 4, "sine_c")
-        y2 = second_product(2 * Q, 2)
-        damping(1, 3 * Q, S, "sq0_256")
-        features(1, sums1[3], 3 * Q, S, "sine_b", h1_bf[:, 1536:2048])
-        place(y2, 2 * Q, 0, 2, "y2")
-        place(y2, 2 * Q, 2, 4, "sine_b")
-        y3 = second_product(3 * Q, 3)
-        place(y3, 3 * Q, 0, 4, "y3")
+        features(1, sums12, HALF, S, "sine_c", h1_bf[:, 1024:2048])
+        place(y1[:, Q:], Q, HALF, 1, 4, "sine_c")
+        for pair in range(2):
+            y2 = second_product(HALF, S, 2 * pair, 2 * pair + 2, 2 + pair)
+            place(y2[:], HALF, S, 2 * pair, 2 * pair + 2, "y2_%d" % pair)
         for n in range(N // P):
             nc.sync.dma_start(out=out[n * P : (n + 1) * P, :], in_=pages[n][:])

@@ -82,6 +82,21 @@ def tile_list_rack_patch_features_kernel(
             planes[name] = sb("plane_" + name, [P, KP], U8)
             nc.vector.quantize_mx(out=codes[name][:].bitcast(E4M3), scales=planes[name][:], in_=grouped[:])
 
+        def quantise_weight_in_halves(name):
+            grouped = keep.tile([P, KP * PACK], BF16, name="grouped_" + name, tag="bf_" + name, align_bytes=64)
+            dst = grouped[:].rearrange("p (t m j) -> p m j t", t=PACK, j=PACK)
+            src = raw[name][:].rearrange("p j (m t) -> p m j t", t=PACK)
+            codes[name] = sb("codes_" + name, [P, KP], U32)
+            planes[name] = sb("plane_" + name, [P, KP], U8)
+            for t in range(0, PACK, 2):
+                nc.vector.tensor_copy(out=dst[:, :, :, t : t + 2], in_=src[:, :, :, t : t + 2])
+            for t in range(0, PACK, 2):
+                cols = slice(t * P, (t + 2) * P)
+                nc.vector.quantize_mx(
+                    out=codes[name][:, cols].bitcast(E4M3), scales=planes[name][:, cols],
+                    in_=grouped[:, PACK * t * P : PACK * (t + 2) * P],
+                )
+
         def words_of(dram, a):
             return dram[a].rearrange("p t i -> p (t i)").bitcast(I32)
 
@@ -105,10 +120,10 @@ def tile_list_rack_patch_features_kernel(
         load_tab_scales(0)
         load_tab_scales(1)
         load_weight("w3_1", w3, 0, 1)
-        nc.sync.dma_start(out=tab_w[0][:].bitcast(I32), in_=words_of(tab_words, 0))
         load_scale_rows(w2_s, w2_scales, range(2))
-        nc.sync.dma_start(out=tab_w[1][:].bitcast(I32), in_=words_of(tab_words, 1))
+        nc.sync.dma_start(out=tab_w[0][:].bitcast(I32), in_=words_of(tab_words, 0))
         load_scale_rows(w2_s, w2_scales, range(2, 4))
+        nc.sync.dma_start(out=tab_w[1][:].bitcast(I32), in_=words_of(tab_words, 1))
 
         def small(name):
             return sb(name, [P, BLOCKS, PACK], F32)
@@ -190,8 +205,12 @@ def tile_list_rack_patch_features_kernel(
             return ap.rearrange("p (c i t) -> p c t i", i=4, t=PACK)
 
         v_w = [sb("v_w%d" % a, [P, S], U32) for a in range(2)]
-        for a in range(2):
-            nc.vector.tensor_copy(v_w[a][:], tab_w[a][:].indirect(list1[:]))
+        nc.vector.tensor_copy(v_w[0][:], tab_w[0][:].indirect(list1[:]))
+        nc.vector.tensor_copy(
+            out=w2_dealt_s[:].rearrange("p (b t m) -> p b t m", b=BLOCKS, t=PACK),
+            in_=w2_s[:].rearrange("p (b m t) -> p b t m", b=BLOCKS, t=PACK),
+        )
+        nc.vector.tensor_copy(v_w[1][:], tab_w[1][:].indirect(list1[:]))
 
         roots = []
         damp = {}
@@ -222,11 +241,6 @@ def tile_list_rack_patch_features_kernel(
 
         damping(0, 0, HALF, "tab_w1", on_vector=True)
         damping(1, 0, HALF, "damp10")
-
-        nc.vector.tensor_copy(
-            out=w2_dealt_s[:].rearrange("p (b t m) -> p b t m", b=BLOCKS, t=PACK),
-            in_=w2_s[:].rearrange("p (b m t) -> p b t m", b=BLOCKS, t=PACK),
-        )
 
         half_phase = sb("half_phase", [P, BLOCKS, PACK], F32)
         nc.vector.tensor_tensor(half_phase[:], phase_sb[:], half_sign[:], ALU.mult)
@@ -302,7 +316,7 @@ def tile_list_rack_patch_features_kernel(
                 )
 
         for name in ("w1_00", "w1_10", "w1_01", "w1_11"):
-            quantise_weight(name, 0)
+            quantise_weight_in_halves(name)
         Q = QUARTER
         sums00 = first_product(0, 0, HALF, 0)
         sums10 = first_product(1, 0, Q, 4)

import math
from contextlib import ExitStack

import concourse.mybir as mybir

K, M, H, N, T, S, T2 = 1024, 512, 1024, 512, 2048, 512, 1024
FLOPS = 2 * S * (K * H + 2 * M * H + H * N)

F32 = mybir.dt.float32
BF16 = mybir.dt.bfloat16
I32 = mybir.dt.int32
U32 = mybir.dt.uint32
U16 = mybir.dt.uint16
U8 = mybir.dt.uint8
E4M3 = mybir.dt.float8_e4m3fn_x4
E2M1 = mybir.dt.float4_e2m1fn_x4
ACT = mybir.ActivationFunctionType
ALU = mybir.AluOpType

P = 128
PACK = 4
KP = P * PACK
HALF = S // 2
QUARTER = S // 4
BLOCKS = H // KP
TINY = 1e-30


def tile_list_rack_patch_features_kernel(
    tc, tab_words, tab_scales, tab2_words, tab2_scales, offs, offs2, offs3, w1, w2_words, w2_scales,
    w3, w4_words, w4_scales, phase, gain, wgo, page1, out,
):
    nc = tc.nc
    with ExitStack() as ctx:
        keep = ctx.enter_context(tc.tile_pool(name="keep", bufs=1))
        ring = ctx.enter_context(tc.tile_pool(name="ring", bufs=2))
        psum = ctx.enter_context(tc.psum_pool(name="psum", bufs=1))

        def sb(name, shape, dtype):
            return keep.tile(shape, dtype, name=name, align_bytes=64)

        list1 = sb("list1", [P, S // 16], U16)
        list2 = sb("list2", [P, S // 16], U16)
        list3 = sb("list3", [P, S // 16], U16)
        tab_w = [keep.tile([P, T], U32, name="tab_w", tag="tab_w%d" % a, align_bytes=64) for a in range(2)]
        tab2_w = sb("tab2_w", [P, T], U32)
        tab_s = sb("tab_s", [P, T], U8)
        tab2_s = sb("tab2_s", [P, T], U8)
        w2_w = sb("w2_w", [P, 2 * H], U8)
        w2_s = sb("w2_s", [P, H], U8)
        w4_w = [sb("w4_w%d" % b, [P, N], U32) for b in range(BLOCKS)]
        w4_s = sb("w4_s", [P, N], U8)
        phase_sb = sb("phase_sb", [P, BLOCKS, PACK], F32)
        gain_sb = sb("gain_sb", [P, BLOCKS, PACK], F32)
        wgo_sb = sb("wgo_sb", [P, S], F32)
        pages = [sb("page%d" % n, [P, T2], F32) for n in range(N // P)]

        nc.vector.memset(tab2_s[:].bitcast(I32), 0)
        nc.vector.memset(tab_s[:].bitcast(I32), 0)
        nc.vector.memset(w2_s[:].bitcast(I32), 0)
        nc.vector.memset(w4_s[:].bitcast(I32), 0)

        raw = {}

        def load_weight(name, w, a, b):
            raw[name] = sb("raw_" + name, [P, PACK, KP], F32)
            rows = w[a * KP : (a + 1) * KP, b * KP : (b + 1) * KP]
            nc.sync.dma_start(out=raw[name][:], in_=rows.rearrange("(p j) c -> p j c", j=PACK))

        codes = {}
        planes = {}

        def quantise_weight(name, scalar_share):
            grouped = keep.tile([P, KP * PACK], BF16, name="grouped_" + name, tag="bf_" + name, align_bytes=64)
            dst = grouped[:].rearrange("p (t m j) -> p m j t", t=PACK, j=PACK)
            src = raw[name][:].rearrange("p j (m t) -> p m j t", t=PACK)
            cut = P - scalar_share
            nc.vector.tensor_copy(out=dst[:, :cut], in_=src[:, :cut])
            if scalar_share:
                nc.scalar.copy(out=dst[:, cut:], in_=src[:, cut:])
            codes[name] = sb("codes_" + name, [P, KP], U32)
            planes[name] = sb("plane_" + name, [P, KP], U8)
            nc.vector.quantize_mx(out=codes[name][:].bitcast(E4M3), scales=planes[name][:], in_=grouped[:])

        def quantise_weight_in_halves(name):
            grouped = keep.tile([P, KP * PACK], BF16, name="grouped_" + name, tag="bf_" + name, align_bytes=64)
            dst = grouped[:].rearrange("p (t m j) -> p m j t", t=PACK, j=PACK)
            src = raw[name][:].rearrange("p j (m t) -> p m j t", t=PACK)
            codes[name] = sb("codes_" + name, [P, KP], U32)
            planes[name] = sb("plane_" + name, [P, KP], U8)
            for t in range(0, PACK, 2):
                nc.vector.tensor_copy(out=dst[:, :, :, t : t + 2], in_=src[:, :, :, t : t + 2])
            for t in range(0, PACK, 2):
                cols = slice(t * P, (t + 2) * P)
                nc.vector.quantize_mx(
                    out=codes[name][:, cols].bitcast(E4M3), scales=planes[name][:, cols],
                    in_=grouped[:, PACK * t * P : PACK * (t + 2) * P],
                )

        def words_of(dram, a):
            return dram[a].rearrange("p t i -> p (t i)").bitcast(I32)

        def load_scale_rows(tile, scales, rows):
            for r in rows:
                nc.sync.dma_start(out=tile[r:P:32, :].bitcast(I32), in_=scales[0, r:16:4, :].bitcast(I32))

        def load_tab_scales(a):
            for e in range(2):
                nc.sync.dma_start(
                    out=tab_s[4 * a + e : P : 16, :].bitcast(I32), in_=tab_scales[a, e:16:2, :].bitcast(I32)
                )

        nc.sync.dma_start(list2[:], offs2)
        nc.sync.dma_start(out=gain_sb[:], in_=gain.rearrange("(b p t) -> p b t", p=P, t=PACK))
        nc.sync.dma_start(list1[:], offs)
        load_weight("w3_0", w3, 0, 0)
        load_scale_rows(tab2_s, tab2_scales, range(4))
        nc.sync.dma_start(out=w2_w[:].bitcast(I32), in_=w2_words[0].bitcast(I32))
        nc.sync.dma_start(out=tab2_w[:].bitcast(I32), in_=words_of(tab2_words, 0))
        load_tab_scales(0)
        load_tab_scales(1)
        load_weight("w3_1", w3, 0, 1)
        load_scale_rows(w2_s, w2_scales, range(2))
        nc.sync.dma_start(out=tab_w[0][:].bitcast(I32), in_=words_of(tab_words, 0))
        load_scale_rows(w2_s, w2_scales, range(2, 4))
        nc.sync.dma_start(out=tab_w[1][:].bitcast(I32), in_=words_of(tab_words, 1))

        def small(name):
            return sb(name, [P, BLOCKS, PACK], F32)

        half_sign = small("half_sign")
        nc.gpsimd.tensor_scalar(half_sign[:], gain_sb[:], 0.0, -0.5, ALU.is_ge, ALU.add)
        half_gain = small("half_gain")
        nc.gpsimd.tensor_tensor(half_gain[:], gain_sb[:], half_sign[:], ALU.mult)
        twice_gain = small("twice_gain")
        nc.gpsimd.tensor_scalar(twice_gain[:], half_gain[:], 4.0, TINY, ALU.mult, ALU.max)
        gain_root = keep.tile([P, BLOCKS, PACK], F32, name="gain_root", tag="bf_w3_0", align_bytes=64)
        nc.scalar.activation(gain_root[:], twice_gain[:], ACT.Abs_reciprocal_sqrt)
        guess = small("guess")
        nc.gpsimd.tensor_tensor(guess[:], gain_root[:], gain_root[:], ALU.mult)
        near_one = small("near_one")
        nc.gpsimd.tensor_tensor(near_one[:], guess[:], twice_gain[:], ALU.mult)
        mend = small("mend")
        nc.gpsimd.tensor_scalar(mend[:], near_one[:], -1.0, 2.0, ALU.mult, ALU.add)
        inv_gain = small("inv_gain")
        nc.gpsimd.tensor_tensor(inv_gain[:], guess[:], mend[:], ALU.mult)

        v2_w = sb("v2_w", [P, S], U32)
        v2_s = sb("v2_s", [P, S], U8)
        nc.vector.tensor_copy(v2_s[:], tab2_s[:].indirect(list2[:]))
        quantise_weight("w3_0", 64)
        nc.vector.tensor_copy(v2_w[:], tab2_w[:].indirect(list2[:]))
        picked_s = sb("picked_s", [P, S], U8)
        nc.vector.tensor_copy(picked_s[:], tab_s[:].indirect(list1[:]))
        v_s = sb("v_s", [P, S], U8)
        nc.vector.tensor_copy(v_s[:].bitcast(I32), picked_s[:].bitcast(I32))

        def move_odd_row(a, e):
            nc.sync.dma_start(
                out=v_s[4 * a + 2 + e : P : 32, :].bitcast(I32),
                in_=picked_s[16 + 4 * a + e : P : 32, :].bitcast(I32),
            )

        def load_w4_scales(quadrants):
            for d in quadrants:
                nc.sync.dma_start(
                    out=w4_s[32 * d : 32 * d + 8, :].bitcast(I32), in_=w4_scales[:, 4 * d : 4 * d + 4, :].bitcast(I32)
                )

        move_odd_row(0, 0)
        load_weight("w1_00", w1, 0, 0)
        move_odd_row(0, 1)
        move_odd_row(1, 0)
        load_weight("w1_10", w1, 1, 0)
        move_odd_row(1, 1)
        nc.sync.dma_start(out=phase_sb[:], in_=phase.rearrange("(b p t) -> p b t", p=P, t=PACK))

        w2_dealt = sb("w2_dealt", [P, 2 * H], U8)
        w2_dealt_s = sb("w2_dealt_s", [P, H], U8)
        nc.scalar.copy(
            out=w2_dealt[:].bitcast(U16).rearrange("p (b t m) -> p b t m", b=BLOCKS, t=PACK),
            in_=w2_w[:].bitcast(U16).rearrange("p (b m t) -> p b t m", b=BLOCKS, t=PACK),
        )
        quantise_weight("w3_1", 0)

        load_weight("w1_01", w1, 0, 1)
        load_w4_scales(range(2))
        load_weight("w1_11", w1, 1, 1)
        load_w4_scales(range(2, 4))
        for b in range(BLOCKS):
            nc.sync.dma_start(out=w4_w[b][:].bitcast(I32), in_=words_of(w4_words, b))
        nc.sync.dma_start(list3[:], offs3)
        for n in range(N // P):
            nc.sync.dma_start(out=pages[n][:], in_=page1[n * P : (n + 1) * P, :])
            if n == 0:
                nc.sync.dma_start(out=wgo_sb[:], in_=wgo)

        def bank(i):
            return psum.tile([P, S], F32, name="bank", tag="bank%d" % i)

        def planar(ap):
            return ap.rearrange("p t (c i) -> p c t i", i=4)

        def woven(ap):
            return ap.rearrange("p (c i t) -> p c t i", i=4, t=PACK)

        v_w = [sb("v_w%d" % a, [P, S], U32) for a in range(2)]
        nc.vector.tensor_copy(v_w[0][:], tab_w[0][:].indirect(list1[:]))
        nc.vector.tensor_copy(
            out=w2_dealt_s[:].rearrange("p (b t m) -> p b t m", b=BLOCKS, t=PACK),
            in_=w2_s[:].rearrange("p (b m t) -> p b t m", b=BLOCKS, t=PACK),
        )
        nc.vector.tensor_copy(v_w[1][:], tab_w[1][:].indirect(list1[:]))

        roots = []
        damp = {}
        for b in range(BLOCKS):
            root = sb("root%d" % b, [P, PACK, S], F32)
            roots.append(root)
            for t in range(PACK):
                cols = slice(t * P, (t + 1) * P)
                d_ps = bank(4 + t)
                nc.tensor.matmul_mx(
                    out=d_ps[:], lhsT=codes["w3_%d" % b][:, cols].bitcast(E4M3), lhsT_scale=planes["w3_%d" % b][:, cols],
                    rhs=v2_w[:].bitcast(E4M3), rhs_scale=v2_s[:], start=True, stop=True,
                )
                d_sq = ring.tile([P, S], F32, name="d_sq", bufs=4)
                nc.scalar.activation(d_sq[:], d_ps[:], ACT.Square)
                inv = inv_gain[:, b, t : t + 1]
                nc.scalar.activation(root[:, t, :], d_sq[:], ACT.Abs_reciprocal_sqrt, bias=inv, scale=inv)

        def damping(b, j0, j1, tag, on_vector=False):
            tile = keep.tile([P, (j1 - j0) * PACK], F32, name="damp", tag=tag, align_bytes=64)
            root = planar(roots[b][:, :, j0:j1])
            if on_vector:
                nc.vector.tensor_tensor(woven(tile[:]), root, root, ALU.mult)
            else:
                nc.scalar.activation(woven(tile[:]), root, ACT.Square)
            for j in range(j0, j1, QUARTER):
                damp[b, j] = tile[:, PACK * (j - j0) :]

        damping(0, 0, HALF, "tab_w1", on_vector=True)
        damping(1, 0, HALF, "damp10")

        half_phase = sb("half_phase", [P, BLOCKS, PACK], F32)
        nc.vector.tensor_tensor(half_phase[:], phase_sb[:], half_sign[:], ALU.mult)
        angle_bias = sb("angle_bias", [P, BLOCKS, PACK], F32)
        nc.vector.tensor_scalar(angle_bias[:], half_phase[:], math.pi / 4, None, ALU.add)

        h_w = [sb("h_w%d" % b, [P, S], U32) for b in range(BLOCKS)]
        h_s = [sb("h_s%d" % b, [P, S], U8) for b in range(BLOCKS)]

        def first_product(b, j0, j1, first_bank):
            width = j1 - j0
            per_bank = S // width
            sums = []
            for g in range(PACK // per_bank):
                acc = bank(first_bank + g)
                ts = range(g * per_bank, (g + 1) * per_bank)
                outs = [acc[:, i * width : (i + 1) * width] for i in range(per_bank)]
                for i, t in enumerate(ts):
                    c0 = b * KP + t * P
                    nc.tensor.matmul_mx(
                        out=outs[i], lhsT=w2_dealt[:, 2 * c0 : 2 * (c0 + P)].bitcast(E2M1),
                        lhsT_scale=w2_dealt_s[:, c0 : c0 + P],
                        rhs=v2_w[:, j0:j1].bitcast(E4M3), rhs_scale=v2_s[:, j0:j1], start=(i == 0), stop=False,
                    )
                for a in range(2):
                    name = "w1_%d%d" % (a, b)
                    for i, t in enumerate(ts):
                        cols = slice(t * P, (t + 1) * P)
                        nc.tensor.matmul_mx(
                            out=outs[i], lhsT=codes[name][:, cols].bitcast(E4M3), lhsT_scale=planes[name][:, cols],
                            rhs=v_w[a][:, j0:j1].bitcast(E4M3), rhs_scale=v_s[4 * a :, j0:j1],
                            start=False, stop=(a == 1 and i == per_bank - 1),
                        )
                sums.extend(outs)
            return sums

        def features(b, sums, j0, j1, sine_tag, rounded):
            width = j1 - j0
            sine = keep.tile([P, PACK, width], F32, name="sine", tag=sine_tag, align_bytes=64)
            for t in range(PACK):
                nc.scalar.activation(
                    sine[:, t, :], sums[t], ACT.Sin, bias=angle_bias[:, b, t : t + 1], scale=half_sign[:, b, t : t + 1]
                )
            sine_sq = keep.tile([P, width * PACK], F32, name="sine_sq", tag="sq%d_%d" % (b, j0), align_bytes=64)
            nc.scalar.activation(woven(sine_sq[:]), planar(sine[:]), ACT.Square)
            nc.vector.scalar_tensor_tensor(
                rounded, sine_sq[:], -0.5, damp[b, j0][:, : PACK * width], ALU.add, ALU.mult
            )
            nc.vector.quantize_mx(out=h_w[b][:, j0:j1].bitcast(E4M3), scales=h_s[b][:, j0:j1], in_=rounded)

        def second_product(j0, j1, n0, n1, bank_index):
            width = j1 - j0
            y_ps = bank(bank_index)
            for n in range(n0, n1):
                cols = slice(n * P, (n + 1) * P)
                for b in range(BLOCKS):
                    nc.tensor.matmul_mx(
                        out=y_ps[:, (n - n0) * width : (n - n0 + 1) * width],
                        lhsT=w4_w[b][:, cols].bitcast(E4M3), lhsT_scale=w4_s[4 * b :, cols],
                        rhs=h_w[b][:, j0:j1].bitcast(E4M3), rhs_scale=h_s[b][:, j0:j1],
                        start=(b == 0), stop=(b == BLOCKS - 1),
                    )
            return y_ps

        def place(values, j0, j1, n0, n1, tag):
            width = j1 - j0
            y_sb = keep.tile([P, (n1 - n0) * width], F32, name="y_sb", tag=tag, align_bytes=64)
            nc.scalar.copy(out=y_sb[:], in_=values)
            for n in range(n0, n1):
                nc.vector.tensor_tensor(
                    pages[n][:].indirect(list3[:, j0 // 16 : j1 // 16]),
                    y_sb[:, (n - n0) * width : (n - n0 + 1) * width], wgo_sb[:, j0:j1], ALU.mult,
                )

        for name in ("w1_00", "w1_10", "w1_01", "w1_11"):
            quantise_weight_in_halves(name)
        Q = QUARTER
        sums00 = first_product(0, 0, HALF, 0)
        sums10 = first_product(1, 0, Q, 4)
        sums11 = first_product(1, Q, HALF, 5)
        sums01 = first_product(0, HALF, S, 2)
        sums12 = first_product(1, HALF, S, 6)
        h0_bf = keep.tile([P, S * PACK], BF16, name="h0_bf", tag="bf_w1_11", align_bytes=64)
        h1_bf = sb("h1_bf", [P, S * PACK], BF16)
        features(0, sums00, 0, HALF, "sine_a", h0_bf[:, 0:1024])
        damping(0, HALF, S, "damp01")
        features(1, sums10, 0, Q, "sine_b", h1_bf[:, 0:512])
        damping(1, HALF, S, "sq1_0", on_vector=True)
        y0 = second_product(0, Q, 0, 4, 0)
        features(1, sums11, Q, HALF, "sine_a", h1_bf[:, 512:1024])
        place(y0[:], 0, Q, 0, 4, "y0")
        y1 = second_product(Q, HALF, 0, 4, 1)
        place(y1[:, :Q], Q, HALF, 0, 1, "y1")
        features(0, sums01, HALF, S, "sine_b", h0_bf[:, 1024:2048])
        features(1, sums12, HALF, S, "sine_c", h1_bf[:, 1024:2048])
        place(y1[:, Q:], Q, HALF, 1, 4, "sine_c")
        for pair in range(2):
            y2 = second_product(HALF, S, 2 * pair, 2 * pair + 2, 2 + pair)
            place(y2[:], HALF, S, 2 * pair, 2 * pair + 2, "y2_%d" % pair)
        for n in range(N // P):
            nc.sync.dma_start(out=out[n * P : (n + 1) * P, :], in_=pages[n][:])
